import numpy as np
import ml_dtypes


def mxq(x, axis, fmt="e4m3"):
    dtype, down = {"e4m3": (ml_dtypes.float8_e4m3fn, 7), "e5m2": (ml_dtypes.float8_e5m2, 14)}[fmt]
    v = np.moveaxis(np.asarray(x, np.float32).astype(ml_dtypes.bfloat16).astype(np.float64), axis, -1)
    blocks = v.reshape(v.shape[:-1] + (-1, 32))
    amax = np.abs(blocks).max(-1, keepdims=True)
    byte = np.maximum(np.where(amax > 0, np.frexp(amax)[1] - 1 + 127, 0) - down, 1)
    scale = np.exp2(byte - 127.0)
    codes = (blocks / scale).astype(np.float32).astype(dtype).astype(np.float64)
    return np.moveaxis((codes * scale).reshape(v.shape), -1, axis)


WIDE = False


def mx_kscale(k):
    if not WIDE:
        return np.ones(k)
    levels = np.array([10, -10, 5, -5, 0])
    if k % 512:
        return np.exp2(np.random.permutation(np.resize(levels, k // 32))).repeat(32)
    a = np.empty((k // 512, 16))
    for p in range(k // 512):
        a[p, :8] = np.random.permutation(np.resize(levels, 8))
        for g in range(8):
            far = levels[np.abs(levels - a[p, g]) >= 10]
            a[p, g + 8] = far[np.random.randint(len(far))]
    return np.exp2(a.ravel()).repeat(32)


def f64(x):
    return np.asarray(x).astype(np.float64)


def striped(idx):
    return np.tile(np.asarray(idx).reshape(-1, 16).T, (8, 1)).astype(np.uint16)


def unstriped(offs):
    return offs[:16].T.reshape(-1).astype(np.int64)


def striped8(idx):
    return np.asarray(idx).reshape(8, -1, 16).transpose(0, 2, 1).reshape(128, -1).astype(np.uint16)


def unstriped8(offs):
    return offs.reshape(8, 16, -1).transpose(0, 2, 1).reshape(8, -1).astype(np.int64)


def pick8(x, idx, run):
    r = np.arange(len(x))
    return x[r[:, None], idx[r % (8 * run) // run]]


E2M1 = np.array([0.0, 0.5, 1.0, 1.5, 2.0, 3.0, 4.0, 6.0, -0.0, -0.5, -1.0, -1.5, -2.0, -3.0, -4.0, -6.0])


def pack_weight(w, fmt):
    k, n = w.shape
    w = f64(np.asarray(w, np.float32).astype(ml_dtypes.bfloat16)).reshape(k // 32, 32, n)
    amax = np.abs(w).max(1)
    if fmt == "e4m3":
        byte = np.frexp(amax)[1] - 1 + 127 - 7
    else:
        mant, ex = np.frexp(amax / 6.0)
        byte = np.where(mant > 0.5, ex, ex - 1) + 127
    byte = np.clip(np.where(amax > 0, byte, 1), 1, 254)
    scaled = (w * np.exp2(127.0 - byte)[:, None, :]).reshape(k, n).astype(np.float32)
    by_word = np.ascontiguousarray(scaled.reshape(k // 512, 128, 4, n).transpose(0, 1, 3, 2))
    if fmt == "e4m3":
        words = by_word.astype(ml_dtypes.float8_e4m3fn).view(np.uint8)
    else:
        c = by_word.astype(ml_dtypes.float4_e2m1fn).view(np.uint8) & 0xF
        words = (c[..., 0::2] | (c[..., 1::2] << 4)).reshape(k // 512, 128, 2 * n)
    return np.ascontiguousarray(words), np.ascontiguousarray(byte.astype(np.uint8).reshape(k // 512, 16, n))


def unpack_weight(words, scales, fmt):
    g, _, n = scales.shape
    words = np.ascontiguousarray(words).reshape(g, 128, n, -1)
    if fmt == "e4m3":
        vals = words.view(ml_dtypes.float8_e4m3fn).astype(np.float64)
    else:
        nib = np.empty((g, 128, n, 4), np.uint8)
        nib[..., 0::2] = words & 0xF
        nib[..., 1::2] = words >> 4
        vals = E2M1[nib]
    vals = vals * np.repeat(np.exp2(scales.astype(np.float64) - 127.0), 8, axis=1)[..., None]
    return vals.transpose(0, 1, 3, 2).reshape(g * 512, n)


K, J, R, T, Z, M, O, C, N, S = 512, 512, 512, 2048, 512, 1024, 256, 512, 256, 1024


def setup_inputs():
    n = np.random.standard_normal
    idx = np.random.permutation(T)[:J]
    idx2 = np.random.permutation(M)[:J]
    idx3 = np.stack([np.random.permutation(J)[:O] for _ in range(8)])
    idx4 = np.stack([np.random.permutation(J)[:O] for _ in range(8)])
    idx5 = np.stack([np.random.permutation(C)[:O] for _ in range(8)])
    idx6 = np.stack([np.random.permutation(C)[:O] for _ in range(8)])
    idx7 = np.random.permutation(S)[:N]
    fk = mx_kscale(K)
    fr = mx_kscale(R)
    fz = mx_kscale(Z)
    xtp = pack_weight(n((K, T)) * fk[:, None], "e2m1")
    wp = pack_weight(n((K, R)) * 1 / np.sqrt(K) / fk[:, None] * fr, "e4m3")
    xop = pack_weight(n((Z, M)) / fz[:, None], "e4m3")
    w2p = pack_weight(n((Z, R)) * 1 / np.sqrt(Z) * fz[:, None] * fr, "e2m1")
    vsp = pack_weight(n((R, S)) * 1 / np.sqrt(R) / fr[:, None], "e2m1")
    return {
        "xt_words": xtp[0],
        "xt_scales": xtp[1],
        "w_words": wp[0],
        "w_scales": wp[1],
        "xo_words": xop[0],
        "xo_scales": xop[1],
        "w2_words": w2p[0],
        "w2_scales": w2p[1],
        "sa": (np.random.uniform(0.5, 1.6, (R, 1))).astype(np.float32),
        "sb": (np.random.uniform(0.5, 1.6, (R, 1))).astype(np.float32),
        "vs_words": vsp[0],
        "vs_scales": vsp[1],
        "offs": striped(idx),
        "offs2": striped(idx2),
        "offs3": striped8(idx3),
        "offs4": striped8(idx4),
        "offs5": striped8(idx5),
        "offs6": striped8(idx6),
        "offs7": striped(idx7),
    }


def reference(xt_words, xt_scales, w_words, w_scales, xo_words, xo_scales, w2_words, w2_scales, sa, sb, vs_words, vs_scales, offs, offs2, offs3, offs4, offs5, offs6, offs7):
    idx = unstriped(offs)
    idx2 = unstriped(offs2)
    idx3 = unstriped8(offs3)
    idx4 = unstriped8(offs4)
    idx5 = unstriped8(offs5)
    idx6 = unstriped8(offs6)
    idx7 = unstriped(offs7)
    xtu = unpack_weight(xt_words, xt_scales, "e2m1")
    wu = unpack_weight(w_words, w_scales, "e4m3")
    xou = unpack_weight(xo_words, xo_scales, "e4m3")
    w2u = unpack_weight(w2_words, w2_scales, "e2m1")
    vsu = unpack_weight(vs_words, vs_scales, "e2m1")
    xtidxg = xtu[:, idx]
    xoidx2g = xou[:, idx2]
    a = wu.T @ xtidxg + w2u.T @ xoidx2g
    f1 = pick8(a, idx3, 64) * f64(sa)
    f2 = pick8(a, idx4, 64) * f64(sb)
    lo = np.minimum(f1, f2)
    hi = np.maximum(f1, f2)
    pl = np.zeros((R, C))
    pl[np.arange(R)[:, None], idx5[np.arange(R) % 512 // 64]] = lo
    pu = np.zeros((R, C))
    pu[np.arange(R)[:, None], idx6[np.arange(R) % 512 // 64]] = hi
    hid = pl + pu
    vsidx7g = vsu[:, idx7]
    hidq = mxq(hid, 0, "e4m3")
    y = vsidx7g.T @ hidq
    return y

@@ -1,0 +1,197 @@
+from contextlib import ExitStack
+
+import concourse.mybir as mybir
+
+K, J, R, T, Z, M, O, C, N, S = 512, 512, 512, 2048, 512, 1024, 256, 512, 256, 1024
+FLOPS = 2 * (K * R * J + Z * R * J + R * N * C)
+
+F32 = mybir.dt.float32
+BF16 = mybir.dt.bfloat16
+I32 = mybir.dt.int32
+U32 = mybir.dt.uint32
+U16 = mybir.dt.uint16
+U8 = mybir.dt.uint8
+FP8X4 = mybir.dt.float8_e4m3fn_x4
+FP4X4 = mybir.dt.float4_e2m1fn_x4
+COPY = mybir.ActivationFunctionType.Copy
+ALU = mybir.AluOpType
+
+P = 128
+PACK = 4
+CHUNK = 128
+CHUNKS = C // CHUNK
+
+
+def tile_picked_tokens_plain_bank_compareexchange_store_plain_kernel(
+    tc, xt_words, xt_scales, w_words, w_scales, xo_words, xo_scales, w2_words, w2_scales,
+    sa, sb, vs_words, vs_scales, offs, offs2, offs3, offs4, offs5, offs6, offs7, out,
+):
+    nc = tc.nc
+    with ExitStack() as ctx:
+        keep = ctx.enter_context(tc.tile_pool(name="keep", bufs=1))
+        psum = ctx.enter_context(tc.psum_pool(name="psum", bufs=1))
+
+        def tile(name, shape, dtype, tag=None):
+            return keep.tile(shape, dtype, name=name, tag=tag or name, align_bytes=64)
+
+        def load_list(name, src):
+            t = keep.tile(list(src.shape), U16, name=name, tag=name)
+            nc.sync.dma_start(t[:], src)
+            return t
+
+        def load_words(name, src, cols, dtype, tag=None):
+            t = tile(name, [P, cols], dtype, tag)
+            nc.sync.dma_start(t[:].bitcast(I32), src.bitcast(I32))
+            return t
+
+        def cleared_plane(name, cols, tag=None):
+            t = tile(name, [P, cols], U8, tag)
+            nc.vector.memset(t[:].bitcast(I32), 0)
+            return t
+
+        def load_plane(t, src):
+            for q in range(4):
+                nc.sync.dma_start(t[32 * q : 32 * q + 4, :].bitcast(I32), src[0, 4 * q : 4 * q + 4, :].bitcast(I32))
+
+        xt_plane = cleared_plane("xt_plane", T)
+        wp = tile("wp", [P, 4, 2 * R], U8)
+        nc.vector.memset(wp[:, 0, :].bitcast(I32), 0)
+        xo_plane = cleared_plane("xo_plane", M)
+        pl = [tile("pl%d" % i, [P, C], F32) for i in range(2)]
+        pu = [tile("pu%d" % i, [P, C], F32) for i in range(2)]
+        for t in (pl[0], pu[0], pl[1], pu[1]):
+            nc.vector.memset(t[:], 0.0)
+
+        l1 = load_list("l1", offs)
+        xt_win = load_words("xt_win", xt_words[0], T, U16)
+        for i, src in enumerate((w_scales, w2_scales)):
+            nc.sync.dma_start(wp[0:4, :, i * R : (i + 1) * R].bitcast(I32), src[0].rearrange("(q i) c -> i q c", i=4).bitcast(I32))
+        load_plane(xt_plane, xt_scales)
+        l2 = load_list("l2", offs2)
+        xo_win = load_words("xo_win", xo_words[0].rearrange("p c r -> p (c r)"), M, U32)
+        load_plane(xo_plane, xo_scales)
+        w_raw = load_words("w_raw", w_words[0].rearrange("p c r -> p (c r)"), R, U32)
+        w2_raw = load_words("w2_raw", w2_words[0], R, U16)
+        l3 = load_list("l3", offs3)
+        sa_t = tile("sa_t", [P, PACK], F32)
+        nc.sync.dma_start(sa_t[:], sa.rearrange("(p t) o -> p (t o)", t=PACK))
+        l4 = load_list("l4", offs4)
+        sb_t = tile("sb_t", [P, PACK], F32)
+        nc.sync.dma_start(sb_t[:], sb.rearrange("(p t) o -> p (t o)", t=PACK))
+        l5 = load_list("l5", offs5)
+        l6 = load_list("l6", offs6)
+        l7 = load_list("l7", offs7)
+
+        for q in range(1, 4):
+            nc.vector.tensor_copy(wp[32 * q : 32 * q + 4, 0, :].bitcast(I32), wp[0:4, q, :].bitcast(I32))
+        wp_dealt = wp[:, 0, :].rearrange("p (i m t) -> p t i m", i=2, t=PACK)
+        ws0 = tile("ws0", [P, 2, P], U8)
+        nc.vector.tensor_copy(ws0[:], wp_dealt[:, 0, :, :])
+
+        xt_g = tile("xt_g", [P, J], U16)
+        xts_g = tile("xts_g", [P, J], U8)
+        xo_g = tile("xo_g", [P, J], U32)
+        nc.vector.tensor_copy(xt_g[:], xt_win[:].indirect(l1[:]))
+        nc.vector.tensor_copy(xts_g[:], xt_plane[:].indirect(l1[:]))
+        nc.vector.tensor_copy(xo_g[:], xo_win[:].indirect(l2[:]))
+
+        w_d = tile("w_d", [P, PACK, P], U32)
+        nc.scalar.copy(w_d[:].rearrange("p t m -> p m t"), w_raw[:].rearrange("p (m t) -> p m t", t=PACK))
+        w2_d = tile("w2_d", [P, PACK, P], U16)
+        nc.scalar.copy(w2_d[:].rearrange("p t m -> p m t"), w2_raw[:].rearrange("p (m t) -> p m t", t=PACK))
+
+        H = J // 2
+        xos_g = tile("xos_g", [P, J], U8)
+        for h in range(2):
+            nc.vector.tensor_copy(xos_g[:, h * H : (h + 1) * H], xo_plane[:].indirect(l2[:, h * 16 : (h + 1) * 16]))
+
+        def first_product(bank, t, ws, w2s, cols):
+            nc.tensor.matmul_mx(out=bank, lhsT=w_d[:, t, :].bitcast(FP8X4), lhsT_scale=ws,
+                                rhs=xt_g[:, cols].bitcast(FP4X4), rhs_scale=xts_g[:, cols], start=True, stop=False)
+            nc.tensor.matmul_mx(out=bank, lhsT=w2_d[:, t, :].bitcast(FP4X4), lhsT_scale=w2s,
+                                rhs=xo_g[:, cols].bitcast(FP8X4), rhs_scale=xos_g[:, cols], start=False, stop=True)
+
+        a = [tile("a%d" % t, [P, J], F32) for t in range(PACK)]
+        for h in range(2):
+            bank = psum.tile([P, H], F32, name="a0h%d" % h, tag="b%d" % h)
+            cols = slice(h * H, (h + 1) * H)
+            first_product(bank[:], 0, ws0[:, 0, :], ws0[:, 1, :], cols)
+            nc.scalar.copy(a[0][:, cols], bank[:])
+
+        wsr = tile("wsr", [P, PACK - 1, 2, P], U8)
+        nc.vector.tensor_copy(wsr[:].rearrange("p t i m -> p i m t"), wp[:, 0, :].rearrange("p (i m t) -> p i m t", i=2, t=PACK)[:, :, :, 1:])
+
+        f1 = [tile("f1_%d" % t, [P, O], F32) for t in range(PACK)]
+        f2 = [tile("f2_%d" % t, [P, O], F32) for t in range(PACK)]
+        lo = [tile("lo_%d" % t, [P, O], F32) for t in range(PACK)]
+        hi = [tile("hi_%d" % t, [P, O], F32) for t in range(PACK)]
+        hid = [tile("hid_%d" % c, [P, CHUNK, PACK], BF16) for c in range(CHUNKS)]
+
+        def make_a(t):
+            bank = psum.tile([P, J], F32, name="a%d_bank" % t, tag="b%d" % (t + 1))
+            first_product(bank[:], t, wsr[:, t - 1, 0, :], wsr[:, t - 1, 1, :], slice(0, J))
+            nc.vector.tensor_copy(a[t][:], bank[:])
+
+        def fetch(t, e0, e1):
+            lc = slice(e0 // 16, e1 // 16)
+            nc.scalar.activation(out=f1[t][:, e0:e1], in_=a[t][:].indirect(l3[:, lc]), func=COPY, scale=sa_t[:, t : t + 1])
+            nc.scalar.activation(out=f2[t][:, e0:e1], in_=a[t][:].indirect(l4[:, lc]), func=COPY, scale=sb_t[:, t : t + 1])
+
+        def pick(dst, op, t, e0, e1):
+            nc.vector.tensor_tensor(dst[t][:, e0:e1], f1[t][:, e0:e1], f2[t][:, e0:e1], op)
+
+        def put(win, lst, src, e0, e1):
+            nc.scalar.activation(out=win[:].indirect(lst[:, e0 // 16 : e1 // 16]), in_=src[:, e0:e1], func=COPY)
+
+        def join(t, c):
+            cols = slice(c * CHUNK, (c + 1) * CHUNK)
+            nc.vector.tensor_tensor(hid[c][:, :, t], pl[t % 2][:, cols], pu[t % 2][:, cols], ALU.add)
+
+        for h in range(2):
+            fetch(0, h * 128, (h + 1) * 128)
+            pick(lo, ALU.min, 0, h * 128, (h + 1) * 128)
+        for h in range(2):
+            put(pl[0], l5, lo[0], h * 128, (h + 1) * 128)
+        make_a(1)
+        pick(hi, ALU.max, 0, 0, O)
+
+        vs_win = load_words("vs_win", vs_words[0], S, U16, tag="xo_win")
+        vs_plane = cleared_plane("vs_plane", S, tag="xo_plane")
+        load_plane(vs_plane, vs_scales)
+        vs_g = tile("vs_g", [P, N], U16)
+        vss_g = tile("vss_g", [P, N], U8)
+
+        for t in range(1, PACK):
+            fetch(t, 0, O)
+            put(pu[(t - 1) % 2], l6, hi[t - 1], 0, O)
+            pick(lo, ALU.min, t, 0, O)
+            put(pl[t % 2], l5, lo[t], 0, O)
+            if t + 1 < PACK:
+                make_a(t + 1)
+            pick(hi, ALU.max, t, 0, O)
+            for c in range(CHUNKS):
+                join(t - 1, c)
+        nc.vector.tensor_copy(vs_g[:], vs_win[:].indirect(l7[:]))
+        nc.vector.tensor_copy(vss_g[:], vs_plane[:].indirect(l7[:]))
+        put(pu[(PACK - 1) % 2], l6, hi[PACK - 1], 0, O)
+
+        out_v = out.rearrange("(u p) c -> p u c", p=P)
+
+        def finish(c):
+            codes = tile("codes%d" % c, [P, CHUNK], U32)
+            scales = tile("scales%d" % c, [P, CHUNK], U8)
+            nc.vector.quantize_mx(out=codes[:].bitcast(FP8X4), scales=scales[:], in_=hid[c][:].rearrange("p c t -> p (c t)"))
+            bank = psum.tile([P, 2, CHUNK], F32, name="y%d" % c, tag="b%d" % ((5 + c) % 8))
+            for u in range(2):
+                ncols = slice(u * P, (u + 1) * P)
+                nc.tensor.matmul_mx(out=bank[:, u, :], lhsT=vs_g[:, ncols].bitcast(FP4X4), lhsT_scale=vss_g[:, ncols],
+                                    rhs=codes[:].bitcast(FP8X4), rhs_scale=scales[:], start=True, stop=True)
+            res = tile("res%d" % c, [P, 2, CHUNK], F32)
+            nc.scalar.copy(res[:], bank[:])
+            nc.sync.dma_start(out_v[:, :, c * CHUNK : (c + 1) * CHUNK], res[:])
+
+        join(PACK - 1, 0)
+        for c in range(CHUNKS):
+            if c + 1 < CHUNKS:
+                join(PACK - 1, c + 1)
+            finish(c)

@@ -53,23 +53,31 @@ def tile_picked_tokens_plain_bank_compareexchange_store_plain_kernel(
             for q in range(4):
                 nc.sync.dma_start(t[32 * q : 32 * q + 4, :].bitcast(I32), src[0, 4 * q : 4 * q + 4, :].bitcast(I32))
 
+        def load_repeated(t, src, cols, queues):
+            for q, queue in enumerate(queues):
+                rows = src[0, 4 * q : 4 * q + 4, :].bitcast(I32)
+                queue.dma_start(t[32 * q : 32 * q + 32, :].bitcast(I32), rows.unsqueeze(0).to_broadcast([8, 4, cols // 4]))
+
         xt_plane = cleared_plane("xt_plane", T)
-        wp = tile("wp", [P, 4, 2 * R], U8)
-        nc.vector.memset(wp[:, 0, :].bitcast(I32), 0)
-        xo_plane = cleared_plane("xo_plane", M)
+        wp = tile("wp", [P, 2, 2 * R], U8)
+        nc.vector.memset(wp[0:64, :, :].bitcast(I32), 0)
         pl = [tile("pl%d" % i, [P, C], F32) for i in range(2)]
         pu = [tile("pu%d" % i, [P, C], F32) for i in range(2)]
-        for t in (pl[0], pu[0], pl[1], pu[1]):
-            nc.vector.memset(t[:], 0.0)
+        for t in (pl[0], pu[0], pl[1]):
+            nc.gpsimd.memset(t[:], 0.0)
+        nc.vector.memset(pu[1][:], 0.0)
 
+        l2 = load_list("l2", offs2)
+        xo_plane = tile("xo_plane", [P, M], U8)
+        load_repeated(xo_plane, xo_scales, M, (nc.sync, nc.sync, nc.scalar, nc.scalar))
         l1 = load_list("l1", offs)
         xt_win = load_words("xt_win", xt_words[0], T, U16)
-        for i, src in enumerate((w_scales, w2_scales)):
-            nc.sync.dma_start(wp[0:4, :, i * R : (i + 1) * R].bitcast(I32), src[0].rearrange("(q i) c -> i q c", i=4).bitcast(I32))
         load_plane(xt_plane, xt_scales)
-        l2 = load_list("l2", offs2)
+        for i, src in enumerate((w_scales, w2_scales)):
+            rows = src[0].rearrange("(h q i) c -> q i h c", h=2, i=4).bitcast(I32)
+            for q in range(2):
+                nc.sync.dma_start(wp[32 * q : 32 * q + 4, :, i * R : (i + 1) * R].bitcast(I32), rows[q])
         xo_win = load_words("xo_win", xo_words[0].rearrange("p c r -> p (c r)"), M, U32)
-        load_plane(xo_plane, xo_scales)
         w_raw = load_words("w_raw", w_words[0].rearrange("p c r -> p (c r)"), R, U32)
         w2_raw = load_words("w2_raw", w2_words[0], R, U16)
         l3 = load_list("l3", offs3)
@@ -82,43 +90,43 @@ def tile_picked_tokens_plain_bank_compareexchange_store_plain_kernel(
         l6 = load_list("l6", offs6)
         l7 = load_list("l7", offs7)
 
-        for q in range(1, 4):
-            nc.vector.tensor_copy(wp[32 * q : 32 * q + 4, 0, :].bitcast(I32), wp[0:4, q, :].bitcast(I32))
-        wp_dealt = wp[:, 0, :].rearrange("p (i m t) -> p t i m", i=2, t=PACK)
-        ws0 = tile("ws0", [P, 2, P], U8)
-        nc.vector.tensor_copy(ws0[:], wp_dealt[:, 0, :, :])
-
         xt_g = tile("xt_g", [P, J], U16)
         xts_g = tile("xts_g", [P, J], U8)
         xo_g = tile("xo_g", [P, J], U32)
+        xos_g = tile("xos_g", [P, J], U8)
+        nc.vector.tensor_copy(xos_g[:], xo_plane[:].indirect(l2[:]))
         nc.vector.tensor_copy(xt_g[:], xt_win[:].indirect(l1[:]))
         nc.vector.tensor_copy(xts_g[:], xt_plane[:].indirect(l1[:]))
-        nc.vector.tensor_copy(xo_g[:], xo_win[:].indirect(l2[:]))
+        nc.vector.tensor_copy(wp[64:128, 0, :].bitcast(I32), wp[0:64, 1, :].bitcast(I32))
+        ws0 = tile("ws0", [P, 2, P], U8)
+        nc.vector.tensor_copy(ws0[:], wp[:, 0, :].rearrange("p (i m t) -> p t i m", i=2, t=PACK)[:, 0, :, :])
 
-        w_d = tile("w_d", [P, PACK, P], U32)
-        nc.scalar.copy(w_d[:].rearrange("p t m -> p m t"), w_raw[:].rearrange("p (m t) -> p m t", t=PACK))
+        w_first = tile("w_first", [P, P], U32)
+        nc.scalar.copy(w_first[:], w_raw[:].rearrange("p (m t) -> p t m", t=PACK)[:, 0, :])
         w2_d = tile("w2_d", [P, PACK, P], U16)
         nc.scalar.copy(w2_d[:].rearrange("p t m -> p m t"), w2_raw[:].rearrange("p (m t) -> p m t", t=PACK))
+        w_rest = tile("w_rest", [P, PACK - 1, P], U32, tag="w2_raw")
+        nc.scalar.copy(w_rest[:].rearrange("p t m -> p m t"), w_raw[:].rearrange("p (m t) -> p m t", t=PACK)[:, :, 1:])
+        w_d = [w_first[:]] + [w_rest[:, t, :] for t in range(PACK - 1)]
 
-        H = J // 2
-        xos_g = tile("xos_g", [P, J], U8)
-        for h in range(2):
-            nc.vector.tensor_copy(xos_g[:, h * H : (h + 1) * H], xo_plane[:].indirect(l2[:, h * 16 : (h + 1) * 16]))
+        pieces = ((0, 256), (256, 384), (384, 512))
+        for e0, e1 in pieces:
+            nc.vector.tensor_copy(xo_g[:, e0:e1], xo_win[:].indirect(l2[:, e0 // 16 : e1 // 16]))
 
         def first_product(bank, t, ws, w2s, cols):
-            nc.tensor.matmul_mx(out=bank, lhsT=w_d[:, t, :].bitcast(FP8X4), lhsT_scale=ws,
+            nc.tensor.matmul_mx(out=bank, lhsT=w_d[t].bitcast(FP8X4), lhsT_scale=ws,
                                 rhs=xt_g[:, cols].bitcast(FP4X4), rhs_scale=xts_g[:, cols], start=True, stop=False)
             nc.tensor.matmul_mx(out=bank, lhsT=w2_d[:, t, :].bitcast(FP4X4), lhsT_scale=w2s,
                                 rhs=xo_g[:, cols].bitcast(FP8X4), rhs_scale=xos_g[:, cols], start=False, stop=True)
 
         a = [tile("a%d" % t, [P, J], F32) for t in range(PACK)]
-        for h in range(2):
-            bank = psum.tile([P, H], F32, name="a0h%d" % h, tag="b%d" % h)
-            cols = slice(h * H, (h + 1) * H)
+        for h, (e0, e1) in enumerate(pieces):
+            bank = psum.tile([P, e1 - e0], F32, name="a0h%d" % h, tag="b%d" % h)
+            cols = slice(e0, e1)
             first_product(bank[:], 0, ws0[:, 0, :], ws0[:, 1, :], cols)
             nc.scalar.copy(a[0][:, cols], bank[:])
 
-        wsr = tile("wsr", [P, PACK - 1, 2, P], U8)
+        wsr = tile("wsr", [P, PACK - 1, 2, P], U8, tag="xo_win")
         nc.vector.tensor_copy(wsr[:].rearrange("p t i m -> p i m t"), wp[:, 0, :].rearrange("p (i m t) -> p i m t", i=2, t=PACK)[:, :, :, 1:])
 
         f1 = [tile("f1_%d" % t, [P, O], F32) for t in range(PACK)]
@@ -128,7 +136,7 @@ def tile_picked_tokens_plain_bank_compareexchange_store_plain_kernel(
         hid = [tile("hid_%d" % c, [P, CHUNK, PACK], BF16) for c in range(CHUNKS)]
 
         def make_a(t):
-            bank = psum.tile([P, J], F32, name="a%d_bank" % t, tag="b%d" % (t + 1))
+            bank = psum.tile([P, J], F32, name="a%d_bank" % t, tag="b%d" % (t + 2))
             first_product(bank[:], t, wsr[:, t - 1, 0, :], wsr[:, t - 1, 1, :], slice(0, J))
             nc.vector.tensor_copy(a[t][:], bank[:])
 
@@ -155,9 +163,9 @@ def tile_picked_tokens_plain_bank_compareexchange_store_plain_kernel(
         make_a(1)
         pick(hi, ALU.max, 0, 0, O)
 
-        vs_win = load_words("vs_win", vs_words[0], S, U16, tag="xo_win")
-        vs_plane = cleared_plane("vs_plane", S, tag="xo_plane")
-        load_plane(vs_plane, vs_scales)
+        vs_win = load_words("vs_win", vs_words[0], S, U16, tag="xt_win")
+        vs_plane = tile("vs_plane", [P, S], U8, tag="xt_plane")
+        load_repeated(vs_plane, vs_scales, S, (nc.sync,) * 4)
         vs_g = tile("vs_g", [P, N], U16)
         vss_g = tile("vss_g", [P, N], U8)
 
@@ -181,7 +189,7 @@ def tile_picked_tokens_plain_bank_compareexchange_store_plain_kernel(
             codes = tile("codes%d" % c, [P, CHUNK], U32)
             scales = tile("scales%d" % c, [P, CHUNK], U8)
             nc.vector.quantize_mx(out=codes[:].bitcast(FP8X4), scales=scales[:], in_=hid[c][:].rearrange("p c t -> p (c t)"))
-            bank = psum.tile([P, 2, CHUNK], F32, name="y%d" % c, tag="b%d" % ((5 + c) % 8))
+            bank = psum.tile([P, 2, CHUNK], F32, name="y%d" % c, tag="b%d" % ((6 + c) % 8))
             for u in range(2):
                 ncols = slice(u * P, (u + 1) * P)
                 nc.tensor.matmul_mx(out=bank[:, u, :], lhsT=vs_g[:, ncols].bitcast(FP4X4), lhsT_scale=vss_g[:, ncols],

@@ -18,7 +18,7 @@ ALU = mybir.AluOpType
 
 P = 128
 PACK = 4
-CHUNK = 128
+CHUNK = 256
 CHUNKS = C // CHUNK
 
 
@@ -39,9 +39,9 @@ def tile_picked_tokens_plain_bank_compareexchange_store_plain_kernel(
             nc.sync.dma_start(t[:], src)
             return t
 
-        def load_words(name, src, cols, dtype, tag=None):
+        def load_words(name, src, cols, dtype, tag=None, queue=nc.sync):
             t = tile(name, [P, cols], dtype, tag)
-            nc.sync.dma_start(t[:].bitcast(I32), src.bitcast(I32))
+            queue.dma_start(t[:].bitcast(I32), src.bitcast(I32))
             return t
 
         def cleared_plane(name, cols, tag=None):
@@ -49,9 +49,8 @@ def tile_picked_tokens_plain_bank_compareexchange_store_plain_kernel(
             nc.vector.memset(t[:].bitcast(I32), 0)
             return t
 
-        def load_plane(t, src):
-            for q in range(4):
-                nc.sync.dma_start(t[32 * q : 32 * q + 4, :].bitcast(I32), src[0, 4 * q : 4 * q + 4, :].bitcast(I32))
+        def load_rows(t, src, q):
+            nc.sync.dma_start(t[32 * q : 32 * q + 4, :].bitcast(I32), src[0, 4 * q : 4 * q + 4, :].bitcast(I32))
 
         def load_repeated(t, src, cols, queues):
             for q, queue in enumerate(queues):
@@ -63,23 +62,25 @@ def tile_picked_tokens_plain_bank_compareexchange_store_plain_kernel(
         nc.vector.memset(wp[0:64, :, :].bitcast(I32), 0)
         pl = [tile("pl%d" % i, [P, C], F32) for i in range(2)]
         pu = [tile("pu%d" % i, [P, C], F32) for i in range(2)]
-        for t in (pl[0], pu[0], pl[1]):
+        w2_raw = load_words("w2_raw", w2_words[0], R, U16, queue=nc.gpsimd)
+        w_raw = load_words("w_raw", w_words[0].rearrange("p c r -> p (c r)"), R, U32, queue=nc.gpsimd)
+        for t in (pl[0], pu[0]):
+            nc.vector.memset(t[:], 0.0)
+        for t in (pl[1], pu[1]):
             nc.gpsimd.memset(t[:], 0.0)
-        nc.vector.memset(pu[1][:], 0.0)
 
         l2 = load_list("l2", offs2)
         xo_plane = tile("xo_plane", [P, M], U8)
         load_repeated(xo_plane, xo_scales, M, (nc.sync, nc.sync, nc.scalar, nc.scalar))
         l1 = load_list("l1", offs)
         xt_win = load_words("xt_win", xt_words[0], T, U16)
-        load_plane(xt_plane, xt_scales)
+        for q in range(4):
+            load_rows(xt_plane, xt_scales, q)
         for i, src in enumerate((w_scales, w2_scales)):
             rows = src[0].rearrange("(h q i) c -> q i h c", h=2, i=4).bitcast(I32)
             for q in range(2):
                 nc.sync.dma_start(wp[32 * q : 32 * q + 4, :, i * R : (i + 1) * R].bitcast(I32), rows[q])
         xo_win = load_words("xo_win", xo_words[0].rearrange("p c r -> p (c r)"), M, U32)
-        w_raw = load_words("w_raw", w_words[0].rearrange("p c r -> p (c r)"), R, U32)
-        w2_raw = load_words("w2_raw", w2_words[0], R, U16)
         l3 = load_list("l3", offs3)
         sa_t = tile("sa_t", [P, PACK], F32)
         nc.sync.dma_start(sa_t[:], sa.rearrange("(p t) o -> p (t o)", t=PACK))
@@ -101,43 +102,43 @@ def tile_picked_tokens_plain_bank_compareexchange_store_plain_kernel(
         ws0 = tile("ws0", [P, 2, P], U8)
         nc.vector.tensor_copy(ws0[:], wp[:, 0, :].rearrange("p (i m t) -> p t i m", i=2, t=PACK)[:, 0, :, :])
 
-        w_first = tile("w_first", [P, P], U32)
-        nc.scalar.copy(w_first[:], w_raw[:].rearrange("p (m t) -> p t m", t=PACK)[:, 0, :])
+        w_d = tile("w_d", [P, PACK, P], U32)
+        nc.scalar.copy(w_d[:].rearrange("p t m -> p m t"), w_raw[:].rearrange("p (m t) -> p m t", t=PACK))
         w2_d = tile("w2_d", [P, PACK, P], U16)
         nc.scalar.copy(w2_d[:].rearrange("p t m -> p m t"), w2_raw[:].rearrange("p (m t) -> p m t", t=PACK))
-        w_rest = tile("w_rest", [P, PACK - 1, P], U32, tag="w2_raw")
-        nc.scalar.copy(w_rest[:].rearrange("p t m -> p m t"), w_raw[:].rearrange("p (m t) -> p m t", t=PACK)[:, :, 1:])
-        w_d = [w_first[:]] + [w_rest[:, t, :] for t in range(PACK - 1)]
 
         pieces = ((0, 256), (256, 384), (384, 512))
         for e0, e1 in pieces:
             nc.vector.tensor_copy(xo_g[:, e0:e1], xo_win[:].indirect(l2[:, e0 // 16 : e1 // 16]))
 
-        def first_product(bank, t, ws, w2s, cols):
-            nc.tensor.matmul_mx(out=bank, lhsT=w_d[t].bitcast(FP8X4), lhsT_scale=ws,
+        def token_pass(bank, t, ws, cols):
+            nc.tensor.matmul_mx(out=bank, lhsT=w_d[:, t, :].bitcast(FP8X4), lhsT_scale=ws,
                                 rhs=xt_g[:, cols].bitcast(FP4X4), rhs_scale=xts_g[:, cols], start=True, stop=False)
+
+        def note_pass(bank, t, w2s, cols):
             nc.tensor.matmul_mx(out=bank, lhsT=w2_d[:, t, :].bitcast(FP4X4), lhsT_scale=w2s,
                                 rhs=xo_g[:, cols].bitcast(FP8X4), rhs_scale=xos_g[:, cols], start=False, stop=True)
 
         a = [tile("a%d" % t, [P, J], F32) for t in range(PACK)]
-        for h, (e0, e1) in enumerate(pieces):
-            bank = psum.tile([P, e1 - e0], F32, name="a0h%d" % h, tag="b%d" % h)
-            cols = slice(e0, e1)
-            first_product(bank[:], 0, ws0[:, 0, :], ws0[:, 1, :], cols)
-            nc.scalar.copy(a[0][:, cols], bank[:])
+        banks = [psum.tile([P, e1 - e0], F32, name="a0h%d" % h, tag="b%d" % h) for h, (e0, e1) in enumerate(pieces)]
+        for bank, (e0, e1) in zip(banks, pieces):
+            token_pass(bank[:], 0, ws0[:, 0, :], slice(e0, e1))
+        for bank, (e0, e1) in zip(banks, pieces):
+            note_pass(bank[:], 0, ws0[:, 1, :], slice(e0, e1))
+            nc.scalar.copy(a[0][:, e0:e1], bank[:])
 
-        wsr = tile("wsr", [P, PACK - 1, 2, P], U8, tag="xo_win")
-        nc.vector.tensor_copy(wsr[:].rearrange("p t i m -> p i m t"), wp[:, 0, :].rearrange("p (i m t) -> p i m t", i=2, t=PACK)[:, :, :, 1:])
-
+        chain = ("xo_win", "ws0", "a0")
         f1 = [tile("f1_%d" % t, [P, O], F32) for t in range(PACK)]
         f2 = [tile("f2_%d" % t, [P, O], F32) for t in range(PACK)]
         lo = [tile("lo_%d" % t, [P, O], F32) for t in range(PACK)]
-        hi = [tile("hi_%d" % t, [P, O], F32) for t in range(PACK)]
-        hid = [tile("hid_%d" % c, [P, CHUNK, PACK], BF16) for c in range(CHUNKS)]
+        hi = {}
 
         def make_a(t):
-            bank = psum.tile([P, J], F32, name="a%d_bank" % t, tag="b%d" % (t + 2))
-            first_product(bank[:], t, wsr[:, t - 1, 0, :], wsr[:, t - 1, 1, :], slice(0, J))
+            ws = tile("ws%d" % t, [P, 2, P], U8, tag=chain[t - 1])
+            nc.vector.tensor_copy(ws[:], wp[:, 0, :].rearrange("p (i m t) -> p t i m", i=2, t=PACK)[:, t, :, :])
+            bank = psum.tile([P, J], F32, name="a%d_bank" % t, tag="b%d" % (t - 1))
+            token_pass(bank[:], t, ws[:, 0, :], slice(0, J))
+            note_pass(bank[:], t, ws[:, 1, :], slice(0, J))
             nc.vector.tensor_copy(a[t][:], bank[:])
 
         def fetch(t, e0, e1):
@@ -161,13 +162,15 @@ def tile_picked_tokens_plain_bank_compareexchange_store_plain_kernel(
         for h in range(2):
             put(pl[0], l5, lo[0], h * 128, (h + 1) * 128)
         make_a(1)
+        hi[0] = tile("hi_0", [P, O], F32, tag=chain[0])
         pick(hi, ALU.max, 0, 0, O)
 
         vs_win = load_words("vs_win", vs_words[0], S, U16, tag="xt_win")
         vs_plane = tile("vs_plane", [P, S], U8, tag="xt_plane")
         load_repeated(vs_plane, vs_scales, S, (nc.sync,) * 4)
-        vs_g = tile("vs_g", [P, N], U16)
-        vss_g = tile("vss_g", [P, N], U8)
+        vs_g = tile("vs_g", [P, N], U16, tag=chain[0])
+        vss_g = tile("vss_g", [P, N], U8, tag="lo_1")
+        hid = [tile("hid_%d" % c, [P, CHUNK, PACK], BF16, tag="f%d_1" % (c + 1)) for c in range(CHUNKS)]
 
         for t in range(1, PACK):
             fetch(t, 0, O)
@@ -176,6 +179,7 @@ def tile_picked_tokens_plain_bank_compareexchange_store_plain_kernel(
             put(pl[t % 2], l5, lo[t], 0, O)
             if t + 1 < PACK:
                 make_a(t + 1)
+            hi[t] = tile("hi_%d" % t, [P, O], F32, tag=chain[t] if t + 1 < PACK else None)
             pick(hi, ALU.max, t, 0, O)
             for c in range(CHUNKS):
                 join(t - 1, c)
@@ -183,23 +187,25 @@ def tile_picked_tokens_plain_bank_compareexchange_store_plain_kernel(
         nc.vector.tensor_copy(vss_g[:], vs_plane[:].indirect(l7[:]))
         put(pu[(PACK - 1) % 2], l6, hi[PACK - 1], 0, O)
 
-        out_v = out.rearrange("(u p) c -> p u c", p=P)
-
-        def finish(c):
-            codes = tile("codes%d" % c, [P, CHUNK], U32)
-            scales = tile("scales%d" % c, [P, CHUNK], U8)
-            nc.vector.quantize_mx(out=codes[:].bitcast(FP8X4), scales=scales[:], in_=hid[c][:].rearrange("p c t -> p (c t)"))
-            bank = psum.tile([P, 2, CHUNK], F32, name="y%d" % c, tag="b%d" % ((6 + c) % 8))
-            for u in range(2):
-                ncols = slice(u * P, (u + 1) * P)
-                nc.tensor.matmul_mx(out=bank[:, u, :], lhsT=vs_g[:, ncols].bitcast(FP4X4), lhsT_scale=vss_g[:, ncols],
-                                    rhs=codes[:].bitcast(FP8X4), rhs_scale=scales[:], start=True, stop=True)
-            res = tile("res%d" % c, [P, 2, CHUNK], F32)
-            nc.scalar.copy(res[:], bank[:])
-            nc.sync.dma_start(out_v[:, :, c * CHUNK : (c + 1) * CHUNK], res[:])
-
-        join(PACK - 1, 0)
+        last = PACK - 1
+        half = CHUNK // 2
+        sums = [tile("sum%d" % c, [P, CHUNK], BF16) for c in range(CHUNKS)]
         for c in range(CHUNKS):
-            if c + 1 < CHUNKS:
-                join(PACK - 1, c + 1)
-            finish(c)
+            cols = slice(c * CHUNK, (c + 1) * CHUNK)
+            nc.vector.tensor_tensor(sums[c][:], pl[last % 2][:, cols], pu[last % 2][:, cols], ALU.add)
+            nc.scalar.copy(hid[c][:, :half, last], sums[c][:, :half])
+        for c in range(CHUNKS):
+            nc.vector.tensor_copy(hid[c][:, half:, last], sums[c][:, half:])
+        codes = [tile("codes%d" % c, [P, CHUNK], U32) for c in range(CHUNKS)]
+        scales = [tile("scales%d" % c, [P, CHUNK], U8) for c in range(CHUNKS)]
+        for c in range(CHUNKS):
+            nc.vector.quantize_mx(out=codes[c][:].bitcast(FP8X4), scales=scales[c][:], in_=hid[c][:].rearrange("p c t -> p (c t)"))
+        for c in range(CHUNKS):
+            for u, copy in enumerate((nc.scalar.copy, nc.vector.tensor_copy)):
+                rows = slice(u * P, (u + 1) * P)
+                bank = psum.tile([P, CHUNK], F32, name="y%d_%d" % (c, u), tag="b%d" % (3 + 2 * c + u))
+                nc.tensor.matmul_mx(out=bank[:], lhsT=vs_g[:, rows].bitcast(FP4X4), lhsT_scale=vss_g[:, rows],
+                                    rhs=codes[c][:].bitcast(FP8X4), rhs_scale=scales[c][:], start=True, stop=True)
+                res = tile("res%d_%d" % (c, u), [P, CHUNK], F32)
+                copy(res[:], bank[:])
+                nc.sync.dma_start(out[rows, c * CHUNK : (c + 1) * CHUNK], res[:])

from contextlib import ExitStack

import concourse.mybir as mybir

K, J, R, T, Z, M, O, C, N, S = 512, 512, 512, 2048, 512, 1024, 256, 512, 256, 1024
FLOPS = 2 * (K * R * J + Z * R * J + R * N * C)

F32 = mybir.dt.float32
BF16 = mybir.dt.bfloat16
I32 = mybir.dt.int32
U32 = mybir.dt.uint32
U16 = mybir.dt.uint16
U8 = mybir.dt.uint8
FP8X4 = mybir.dt.float8_e4m3fn_x4
FP4X4 = mybir.dt.float4_e2m1fn_x4
COPY = mybir.ActivationFunctionType.Copy
ALU = mybir.AluOpType

P = 128
PACK = 4
CHUNK = 256
CHUNKS = C // CHUNK


def tile_picked_tokens_plain_bank_compareexchange_store_plain_kernel(
    tc, xt_words, xt_scales, w_words, w_scales, xo_words, xo_scales, w2_words, w2_scales,
    sa, sb, vs_words, vs_scales, offs, offs2, offs3, offs4, offs5, offs6, offs7, out,
):
    nc = tc.nc
    with ExitStack() as ctx:
        keep = ctx.enter_context(tc.tile_pool(name="keep", bufs=1))
        psum = ctx.enter_context(tc.psum_pool(name="psum", bufs=1))

        def tile(name, shape, dtype, tag=None):
            return keep.tile(shape, dtype, name=name, tag=tag or name, align_bytes=64)

        def load_list(name, src):
            t = keep.tile(list(src.shape), U16, name=name, tag=name)
            nc.sync.dma_start(t[:], src)
            return t

        def load_words(name, src, cols, dtype, tag=None, queue=nc.sync):
            t = tile(name, [P, cols], dtype, tag)
            queue.dma_start(t[:].bitcast(I32), src.bitcast(I32))
            return t

        def cleared_plane(name, cols, tag=None):
            t = tile(name, [P, cols], U8, tag)
            nc.vector.memset(t[:].bitcast(I32), 0)
            return t

        def load_rows(t, src, q):
            nc.sync.dma_start(t[32 * q : 32 * q + 4, :].bitcast(I32), src[0, 4 * q : 4 * q + 4, :].bitcast(I32))

        def load_repeated(t, src, cols, queues):
            for q, queue in enumerate(queues):
                rows = src[0, 4 * q : 4 * q + 4, :].bitcast(I32)
                queue.dma_start(t[32 * q : 32 * q + 32, :].bitcast(I32), rows.unsqueeze(0).to_broadcast([8, 4, cols // 4]))

        xt_plane = cleared_plane("xt_plane", T)
        wp = tile("wp", [P, 2, 2 * R], U8)
        nc.vector.memset(wp[0:64, :, :].bitcast(I32), 0)
        pl = [tile("pl%d" % i, [P, C], F32) for i in range(2)]
        pu = [tile("pu%d" % i, [P, C], F32) for i in range(2)]
        w2_raw = load_words("w2_raw", w2_words[0], R, U16, queue=nc.gpsimd)
        w_raw = load_words("w_raw", w_words[0].rearrange("p c r -> p (c r)"), R, U32, queue=nc.gpsimd)
        for t in (pl[0], pu[0]):
            nc.vector.memset(t[:], 0.0)
        for t in (pl[1], pu[1]):
            nc.gpsimd.memset(t[:], 0.0)

        l2 = load_list("l2", offs2)
        xo_plane = tile("xo_plane", [P, M], U8)
        load_repeated(xo_plane, xo_scales, M, (nc.sync, nc.sync, nc.scalar, nc.scalar))
        l1 = load_list("l1", offs)
        xt_win = load_words("xt_win", xt_words[0], T, U16)
        for q in range(4):
            load_rows(xt_plane, xt_scales, q)
        for i, src in enumerate((w_scales, w2_scales)):
            rows = src[0].rearrange("(h q i) c -> q i h c", h=2, i=4).bitcast(I32)
            for q in range(2):
                nc.sync.dma_start(wp[32 * q : 32 * q + 4, :, i * R : (i + 1) * R].bitcast(I32), rows[q])
        xo_win = load_words("xo_win", xo_words[0].rearrange("p c r -> p (c r)"), M, U32)
        l3 = load_list("l3", offs3)
        sa_t = tile("sa_t", [P, PACK], F32)
        nc.sync.dma_start(sa_t[:], sa.rearrange("(p t) o -> p (t o)", t=PACK))
        l4 = load_list("l4", offs4)
        sb_t = tile("sb_t", [P, PACK], F32)
        nc.sync.dma_start(sb_t[:], sb.rearrange("(p t) o -> p (t o)", t=PACK))
        l5 = load_list("l5", offs5)
        l6 = load_list("l6", offs6)
        l7 = load_list("l7", offs7)

        xt_g = tile("xt_g", [P, J], U16)
        xts_g = tile("xts_g", [P, J], U8)
        xo_g = tile("xo_g", [P, J], U32)
        xos_g = tile("xos_g", [P, J], U8)
        nc.vector.tensor_copy(xos_g[:], xo_plane[:].indirect(l2[:]))
        nc.vector.tensor_copy(xt_g[:], xt_win[:].indirect(l1[:]))
        nc.vector.tensor_copy(xts_g[:], xt_plane[:].indirect(l1[:]))
        nc.vector.tensor_copy(wp[64:128, 0, :].bitcast(I32), wp[0:64, 1, :].bitcast(I32))
        ws0 = tile("ws0", [P, 2, P], U8)
        nc.vector.tensor_copy(ws0[:], wp[:, 0, :].rearrange("p (i m t) -> p t i m", i=2, t=PACK)[:, 0, :, :])

        w_d = tile("w_d", [P, PACK, P], U32)
        nc.scalar.copy(w_d[:].rearrange("p t m -> p m t"), w_raw[:].rearrange("p (m t) -> p m t", t=PACK))
        w2_d = tile("w2_d", [P, PACK, P], U16)
        nc.scalar.copy(w2_d[:].rearrange("p t m -> p m t"), w2_raw[:].rearrange("p (m t) -> p m t", t=PACK))

        pieces = ((0, 256), (256, 384), (384, 512))
        for e0, e1 in pieces:
            nc.vector.tensor_copy(xo_g[:, e0:e1], xo_win[:].indirect(l2[:, e0 // 16 : e1 // 16]))

        def token_pass(bank, t, ws, cols):
            nc.tensor.matmul_mx(out=bank, lhsT=w_d[:, t, :].bitcast(FP8X4), lhsT_scale=ws,
                                rhs=xt_g[:, cols].bitcast(FP4X4), rhs_scale=xts_g[:, cols], start=True, stop=False)

        def note_pass(bank, t, w2s, cols):
            nc.tensor.matmul_mx(out=bank, lhsT=w2_d[:, t, :].bitcast(FP4X4), lhsT_scale=w2s,
                                rhs=xo_g[:, cols].bitcast(FP8X4), rhs_scale=xos_g[:, cols], start=False, stop=True)

        a = [tile("a%d" % t, [P, J], F32) for t in range(PACK)]
        banks = [psum.tile([P, e1 - e0], F32, name="a0h%d" % h, tag="b%d" % h) for h, (e0, e1) in enumerate(pieces)]
        for bank, (e0, e1) in zip(banks, pieces):
            token_pass(bank[:], 0, ws0[:, 0, :], slice(e0, e1))
        for bank, (e0, e1) in zip(banks, pieces):
            note_pass(bank[:], 0, ws0[:, 1, :], slice(e0, e1))
            nc.scalar.copy(a[0][:, e0:e1], bank[:])

        chain = ("xo_win", "ws0", "a0")
        f1 = [tile("f1_%d" % t, [P, O], F32) for t in range(PACK)]
        f2 = [tile("f2_%d" % t, [P, O], F32) for t in range(PACK)]
        lo = [tile("lo_%d" % t, [P, O], F32) for t in range(PACK)]
        hi = {}

        def make_a(t):
            ws = tile("ws%d" % t, [P, 2, P], U8, tag=chain[t - 1])
            nc.vector.tensor_copy(ws[:], wp[:, 0, :].rearrange("p (i m t) -> p t i m", i=2, t=PACK)[:, t, :, :])
            bank = psum.tile([P, J], F32, name="a%d_bank" % t, tag="b%d" % (t - 1))
            token_pass(bank[:], t, ws[:, 0, :], slice(0, J))
            note_pass(bank[:], t, ws[:, 1, :], slice(0, J))
            nc.vector.tensor_copy(a[t][:], bank[:])

        def fetch(t, e0, e1):
            lc = slice(e0 // 16, e1 // 16)
            nc.scalar.activation(out=f1[t][:, e0:e1], in_=a[t][:].indirect(l3[:, lc]), func=COPY, scale=sa_t[:, t : t + 1])
            nc.scalar.activation(out=f2[t][:, e0:e1], in_=a[t][:].indirect(l4[:, lc]), func=COPY, scale=sb_t[:, t : t + 1])

        def pick(dst, op, t, e0, e1):
            nc.vector.tensor_tensor(dst[t][:, e0:e1], f1[t][:, e0:e1], f2[t][:, e0:e1], op)

        def put(win, lst, src, e0, e1):
            nc.scalar.activation(out=win[:].indirect(lst[:, e0 // 16 : e1 // 16]), in_=src[:, e0:e1], func=COPY)

        def join(t, c):
            cols = slice(c * CHUNK, (c + 1) * CHUNK)
            nc.vector.tensor_tensor(hid[c][:, :, t], pl[t % 2][:, cols], pu[t % 2][:, cols], ALU.add)

        for h in range(2):
            fetch(0, h * 128, (h + 1) * 128)
            pick(lo, ALU.min, 0, h * 128, (h + 1) * 128)
        for h in range(2):
            put(pl[0], l5, lo[0], h * 128, (h + 1) * 128)
        make_a(1)
        hi[0] = tile("hi_0", [P, O], F32, tag=chain[0])
        pick(hi, ALU.max, 0, 0, O)

        vs_win = load_words("vs_win", vs_words[0], S, U16, tag="xt_win")
        vs_plane = tile("vs_plane", [P, S], U8, tag="xt_plane")
        load_repeated(vs_plane, vs_scales, S, (nc.sync,) * 4)
        vs_g = tile("vs_g", [P, N], U16, tag=chain[0])
        vss_g = tile("vss_g", [P, N], U8, tag="lo_1")
        hid = [tile("hid_%d" % c, [P, CHUNK, PACK], BF16, tag="f%d_1" % (c + 1)) for c in range(CHUNKS)]

        for t in range(1, PACK):
            fetch(t, 0, O)
            put(pu[(t - 1) % 2], l6, hi[t - 1], 0, O)
            pick(lo, ALU.min, t, 0, O)
            put(pl[t % 2], l5, lo[t], 0, O)
            if t + 1 < PACK:
                make_a(t + 1)
            hi[t] = tile("hi_%d" % t, [P, O], F32, tag=chain[t] if t + 1 < PACK else None)
            pick(hi, ALU.max, t, 0, O)
            for c in range(CHUNKS):
                join(t - 1, c)
        nc.vector.tensor_copy(vs_g[:], vs_win[:].indirect(l7[:]))
        nc.vector.tensor_copy(vss_g[:], vs_plane[:].indirect(l7[:]))
        put(pu[(PACK - 1) % 2], l6, hi[PACK - 1], 0, O)

        last = PACK - 1
        half = CHUNK // 2
        sums = [tile("sum%d" % c, [P, CHUNK], BF16) for c in range(CHUNKS)]
        for c in range(CHUNKS):
            cols = slice(c * CHUNK, (c + 1) * CHUNK)
            nc.vector.tensor_tensor(sums[c][:], pl[last % 2][:, cols], pu[last % 2][:, cols], ALU.add)
            nc.scalar.copy(hid[c][:, :half, last], sums[c][:, :half])
        for c in range(CHUNKS):
            nc.vector.tensor_copy(hid[c][:, half:, last], sums[c][:, half:])
        codes = [tile("codes%d" % c, [P, CHUNK], U32) for c in range(CHUNKS)]
        scales = [tile("scales%d" % c, [P, CHUNK], U8) for c in range(CHUNKS)]
        for c in range(CHUNKS):
            nc.vector.quantize_mx(out=codes[c][:].bitcast(FP8X4), scales=scales[c][:], in_=hid[c][:].rearrange("p c t -> p (c t)"))
        for c in range(CHUNKS):
            for u, copy in enumerate((nc.scalar.copy, nc.vector.tensor_copy)):
                rows = slice(u * P, (u + 1) * P)
                bank = psum.tile([P, CHUNK], F32, name="y%d_%d" % (c, u), tag="b%d" % (3 + 2 * c + u))
                nc.tensor.matmul_mx(out=bank[:], lhsT=vs_g[:, rows].bitcast(FP4X4), lhsT_scale=vss_g[:, rows],
                                    rhs=codes[c][:].bitcast(FP8X4), rhs_scale=scales[c][:], start=True, stop=True)
                res = tile("res%d_%d" % (c, u), [P, CHUNK], F32)
                copy(res[:], bank[:])
                nc.sync.dma_start(out[rows, c * CHUNK : (c + 1) * CHUNK], res[:])
